import numpy as np
import ml_dtypes


def mxq(x, axis, fmt="e4m3"):
    dtype, down = {"e4m3": (ml_dtypes.float8_e4m3fn, 7), "e5m2": (ml_dtypes.float8_e5m2, 14)}[fmt]
    v = np.moveaxis(np.asarray(x, np.float32).astype(ml_dtypes.bfloat16).astype(np.float64), axis, -1)
    blocks = v.reshape(v.shape[:-1] + (-1, 32))
    amax = np.abs(blocks).max(-1, keepdims=True)
    byte = np.maximum(np.where(amax > 0, np.frexp(amax)[1] - 1 + 127, 0) - down, 1)
    scale = np.exp2(byte - 127.0)
    codes = (blocks / scale).astype(np.float32).astype(dtype).astype(np.float64)
    return np.moveaxis((codes * scale).reshape(v.shape), -1, axis)


WIDE = False


def mx_kscale(k):
    if not WIDE:
        return np.ones(k)
    levels = np.array([30, -30])
    if k % 512:
        return np.exp2(np.random.permutation(np.resize(levels, k // 32))).repeat(32)
    a = np.empty((k // 512, 16))
    for p in range(k // 512):
        a[p, :8] = np.random.permutation(np.resize(levels, 8))
        for g in range(8):
            far = levels[np.abs(levels - a[p, g]) >= 10]
            a[p, g + 8] = far[np.random.randint(len(far))]
    return np.exp2(a.ravel()).repeat(32)


def f64(x):
    return np.asarray(x).astype(np.float64)


def striped(idx):
    return np.tile(np.asarray(idx).reshape(-1, 16).T, (8, 1)).astype(np.uint16)


def unstriped(offs):
    return offs[:16].T.reshape(-1).astype(np.int64)


def striped8(idx):
    return np.asarray(idx).reshape(8, -1, 16).transpose(0, 2, 1).reshape(128, -1).astype(np.uint16)


def unstriped8(offs):
    return offs.reshape(8, 16, -1).transpose(0, 2, 1).reshape(8, -1).astype(np.int64)


def pick8(x, idx, run):
    r = np.arange(len(x))
    return x[r[:, None], idx[r % (8 * run) // run]]


E2M1 = np.array([0.0, 0.5, 1.0, 1.5, 2.0, 3.0, 4.0, 6.0, -0.0, -0.5, -1.0, -1.5, -2.0, -3.0, -4.0, -6.0])


def pack_weight(w, fmt):
    k, n = w.shape
    w = f64(np.asarray(w, np.float32).astype(ml_dtypes.bfloat16)).reshape(k // 32, 32, n)
    amax = np.abs(w).max(1)
    if fmt == "e4m3":
        byte = np.frexp(amax)[1] - 1 + 127 - 7
    else:
        mant, ex = np.frexp(amax / 6.0)
        byte = np.where(mant > 0.5, ex, ex - 1) + 127
    byte = np.clip(np.where(amax > 0, byte, 1), 1, 254)
    scaled = (w * np.exp2(127.0 - byte)[:, None, :]).reshape(k, n).astype(np.float32)
    by_word = np.ascontiguousarray(scaled.reshape(k // 512, 128, 4, n).transpose(0, 1, 3, 2))
    if fmt == "e4m3":
        words = by_word.astype(ml_dtypes.float8_e4m3fn).view(np.uint8)
    else:
        c = by_word.astype(ml_dtypes.float4_e2m1fn).view(np.uint8) & 0xF
        words = (c[..., 0::2] | (c[..., 1::2] << 4)).reshape(k // 512, 128, 2 * n)
    return np.ascontiguousarray(words), np.ascontiguousarray(byte.astype(np.uint8).reshape(k // 512, 16, n))


def unpack_weight(words, scales, fmt):
    g, _, n = scales.shape
    words = np.ascontiguousarray(words).reshape(g, 128, n, -1)
    if fmt == "e4m3":
        vals = words.view(ml_dtypes.float8_e4m3fn).astype(np.float64)
    else:
        nib = np.empty((g, 128, n, 4), np.uint8)
        nib[..., 0::2] = words & 0xF
        nib[..., 1::2] = words >> 4
        vals = E2M1[nib]
    vals = vals * np.repeat(np.exp2(scales.astype(np.float64) - 127.0), 8, axis=1)[..., None]
    return vals.transpose(0, 1, 3, 2).reshape(g * 512, n)


def sigmoid(v):
    return 1.0 / (1.0 + np.exp(-v))


def sgn(shape):
    return np.random.uniform(0.5, 2.0, shape) * np.where(np.random.standard_normal(shape) < 0, -1.0, 1.0)


K, T, J, R, V, O, N, S = 512, 1024, 256, 512, 1024, 128, 256, 1024


def setup_inputs():
    n = np.random.standard_normal
    idx = np.random.permutation(V)[:R]
    idx2 = np.random.permutation(T)[:J]
    idx3 = np.stack([np.random.permutation(J)[:O] for _ in range(8)])
    idx4 = np.stack([np.random.permutation(J)[:O] for _ in range(8)])
    idx5 = np.random.permutation(S)[:N]
    fk = mx_kscale(K)
    fr = mx_kscale(R)
    xtp = pack_weight(n((K, T)) / fk[:, None], "e2m1")
    wtp = pack_weight(n((K, V)) * 1 / np.sqrt(K) * fk[:, None], "e4m3")
    vsp = pack_weight(n((R, S)) * 1 / np.sqrt(R) / fr[:, None], "e2m1")
    return {
        "xt_words": xtp[0],
        "xt_scales": xtp[1],
        "wt_words": wtp[0],
        "wt_scales": wtp[1],
        "sa": (np.random.uniform(0.5, 1.6, (R, 1)) * fr[:, None]).astype(np.float32),
        "sg": (sgn((R, 1))).astype(np.float32),
        "bg": (np.random.uniform(-2.0, 2.0, (R, 1))).astype(np.float32),
        "vs_words": vsp[0],
        "vs_scales": vsp[1],
        "offs": striped(idx),
        "offs2": striped(idx2),
        "offs3": striped8(idx3),
        "offs4": striped8(idx4),
        "offs5": striped(idx5),
    }


def reference(xt_words, xt_scales, wt_words, wt_scales, sa, sg, bg, vs_words, vs_scales, offs, offs2, offs3, offs4, offs5):
    idx = unstriped(offs)
    idx2 = unstriped(offs2)
    idx3 = unstriped8(offs3)
    idx4 = unstriped8(offs4)
    idx5 = unstriped(offs5)
    xtu = unpack_weight(xt_words, xt_scales, "e2m1")
    wtu = unpack_weight(wt_words, wt_scales, "e4m3")
    vsu = unpack_weight(vs_words, vs_scales, "e2m1")
    wtidxg = wtu[:, idx]
    xtidx2g = xtu[:, idx2]
    a = wtidxg.T @ xtidx2g
    hid = pick8(a, idx3, 64) * f64(sa) * sigmoid(pick8(a, idx4, 64) * f64(sg) + f64(bg))
    vsidx5g = vsu[:, idx5]
    hidq = mxq(hid, 0, "e5m2")
    y = vsidx5g.T @ hidq
    return y

@@ -1,0 +1,151 @@
+from contextlib import ExitStack
+
+import concourse.mybir as mybir
+
+K, T, J, R, V, O, N, S = 512, 1024, 256, 512, 1024, 128, 256, 1024
+FLOPS = 2 * K * R * J + 2 * R * N * O
+
+F32 = mybir.dt.float32
+BF16 = mybir.dt.bfloat16
+I32 = mybir.dt.int32
+U32 = mybir.dt.uint32
+U16 = mybir.dt.uint16
+U8 = mybir.dt.uint8
+E4M3X4 = mybir.dt.float8_e4m3fn_x4
+E5M2X4 = mybir.dt.float8_e5m2_x4
+E2M1X4 = mybir.dt.float4_e2m1fn_x4
+ACT = mybir.ActivationFunctionType
+MULT = mybir.AluOpType.mult
+
+P = 128
+PACK = 4
+QUADS = 4
+
+
+def tile_list_groupgated_chosen_store_plain_kernel(
+    tc, xt_words, xt_scales, wt_words, wt_scales, sa, sg, bg, vs_words, vs_scales, offs, offs2, offs3, offs4, offs5, out
+):
+    nc = tc.nc
+    with ExitStack() as ctx:
+        lists = ctx.enter_context(tc.tile_pool(name="lists", bufs=1))
+        sb = ctx.enter_context(tc.tile_pool(name="sb", bufs=1))
+        ps = ctx.enter_context(tc.psum_pool(name="ps", bufs=1))
+
+        def list_tile(ap, name):
+            return lists.tile([P, ap.shape[1]], U16, name=name)
+
+        l_wt = list_tile(offs, "l_wt")
+        l_xt = list_tile(offs2, "l_xt")
+        l_val = list_tile(offs3, "l_val")
+        l_gate = list_tile(offs4, "l_gate")
+        l_vs = list_tile(offs5, "l_vs")
+
+        wt_w = sb.tile([P, V], U32, name="wt_w", align_bytes=64)
+        xt_w = sb.tile([P, T], U16, name="xt_w", align_bytes=64)
+        vs_w = sb.tile([P, S], U16, name="vs_w", align_bytes=64)
+        wt_s = sb.tile([P, V], U8, name="wt_s", align_bytes=64)
+        xt_s = sb.tile([P, T], U8, name="xt_s", align_bytes=64)
+        vs_s = sb.tile([P, S], U8, name="vs_s", align_bytes=64)
+        for plane in (wt_s, xt_s, vs_s):
+            nc.vector.memset(plane[:].bitcast(I32), 0)
+
+        def load_scale_rows(queue, plane, scales, q):
+            queue.dma_start(
+                out=plane[32 * q : 32 * q + 4, :].bitcast(I32), in_=scales[0, 4 * q : 4 * q + 4, :].bitcast(I32)
+            )
+
+        sg_t = sb.tile([P, PACK], F32, name="sg_t")
+        bg_t = sb.tile([P, PACK], F32, name="bg_t")
+        sa_t = sb.tile([P, PACK], F32, name="sa_t")
+        for tile, vec in ((sg_t, sg), (bg_t, bg), (sa_t, sa)):
+            nc.gpsimd.dma_start(out=tile[:], in_=vec.rearrange("(p t) o -> p (t o)", t=PACK))
+
+        nc.sync.dma_start(l_wt[:], offs)
+        load_scale_rows(nc.sync, wt_s, wt_scales, 0)
+        for q in range(1, QUADS):
+            load_scale_rows(nc.scalar, wt_s, wt_scales, q)
+        nc.sync.dma_start(l_xt[:], offs2)
+        nc.sync.dma_start(out=xt_w[:].bitcast(I32), in_=xt_words[0].bitcast(I32))
+        nc.sync.dma_start(out=wt_w[:].bitcast(I32), in_=wt_words[0].rearrange("p n t -> p (n t)").bitcast(I32))
+        for q in range(QUADS):
+            load_scale_rows(nc.sync, xt_s, xt_scales, q)
+        nc.sync.dma_start(l_gate[:], offs4)
+        nc.sync.dma_start(l_val[:], offs3)
+        nc.sync.dma_start(out=vs_w[:].bitcast(I32), in_=vs_words[0].bitcast(I32))
+        nc.sync.dma_start(l_vs[:], offs5)
+        for q in range(QUADS):
+            load_scale_rows(nc.sync, vs_s, vs_scales, q)
+
+        wg_s = sb.tile([P, PACK, P], U8, name="wg_s", align_bytes=64)
+        wg_w = sb.tile([P, PACK, P], U32, name="wg_w", align_bytes=64)
+        xg_w = sb.tile([P, J], U16, name="xg_w", align_bytes=64)
+        xg_s = sb.tile([P, J], U8, name="xg_s", align_bytes=64)
+        nc.vector.tensor_copy(wg_s[:].rearrange("p t q -> p q t"), wt_s[:].indirect(l_wt[:]))
+        nc.vector.tensor_copy(xg_w[:], xt_w[:].indirect(l_xt[:]))
+        nc.vector.tensor_copy(wg_w[:].rearrange("p t q -> p q t"), wt_w[:].indirect(l_wt[:]))
+        nc.vector.tensor_copy(xg_s[:], xt_s[:].indirect(l_xt[:]))
+
+        a_sb = []
+        for t in range(PACK):
+            a_ps = ps.tile([P, J], F32, name=f"a_ps{t}")
+            nc.tensor.matmul_mx(
+                out=a_ps[:],
+                lhsT=wg_w[:, t, :].bitcast(E4M3X4),
+                lhsT_scale=wg_s[:, t, :],
+                rhs=xg_w[:].bitcast(E2M1X4),
+                rhs_scale=xg_s[:],
+                start=True,
+                stop=True,
+            )
+            a_t = sb.tile([P, J], F32, name=f"a_sb{t}")
+            nc.vector.tensor_copy(a_t[:], a_ps[:])
+            a_sb.append(a_t)
+
+        vg_w = sb.tile([P, N], U16, name="vg_w", align_bytes=64)
+        vg_s = sb.tile([P, N], U8, name="vg_s", align_bytes=64)
+        nc.vector.tensor_copy(vg_w[:], vs_w[:].indirect(l_vs[:]))
+        nc.vector.tensor_copy(vg_s[:], vs_s[:].indirect(l_vs[:]))
+
+        hid = sb.tile([P, O, PACK], BF16, name="hid", align_bytes=64)
+        for u in range(2):
+            gate = sb.tile([P, 2, O], F32, name=f"gate{u}")
+            val = sb.tile([P, 2, O], F32, name=f"val{u}")
+            for e in range(2):
+                t = 2 * u + e
+                nc.scalar.activation(
+                    out=gate[:, e, :], in_=a_sb[t][:].indirect(l_gate[:]), func=ACT.Sigmoid,
+                    bias=bg_t[:, t : t + 1], scale=sg_t[:, t : t + 1],
+                )
+                nc.scalar.activation(
+                    out=val[:, e, :], in_=a_sb[t][:].indirect(l_val[:]), func=ACT.Copy, scale=sa_t[:, t : t + 1]
+                )
+            nc.vector.tensor_tensor(
+                hid[:, :, 2 * u : 2 * u + 2],
+                val[:].rearrange("p e o -> p o e"),
+                gate[:].rearrange("p e o -> p o e"),
+                MULT,
+            )
+
+        hq_w = sb.tile([P, O], U32, name="hq_w", align_bytes=64)
+        hq_s = sb.tile([P, O], U8, name="hq_s", align_bytes=64)
+        nc.vector.quantize_mx(out=hq_w[:].bitcast(E5M2X4), scales=hq_s[:], in_=hid[:].rearrange("p o t -> p (o t)"))
+
+        for h in range(N // P):
+            cols = slice(h * P, (h + 1) * P)
+            y_ps = ps.tile([P, O], F32, name=f"y_ps{h}")
+            nc.tensor.matmul_mx(
+                out=y_ps[:],
+                lhsT=vg_w[:, cols].bitcast(E2M1X4),
+                lhsT_scale=vg_s[:, cols],
+                rhs=hq_w[:].bitcast(E5M2X4),
+                rhs_scale=hq_s[:],
+                start=True,
+                stop=True,
+            )
+            y_sb = sb.tile([P, O], F32, name=f"y_sb{h}")
+            if h == 0:
+                nc.vector.tensor_copy(y_sb[:], y_ps[:])
+                nc.sync.dma_start(out=out[cols, :], in_=y_sb[:])
+            else:
+                nc.scalar.copy(y_sb[:], y_ps[:])
+                nc.scalar.dma_start(out=out[cols, :], in_=y_sb[:])

@@ -44,8 +44,8 @@ def tile_list_groupgated_chosen_store_plain_kernel(
         xt_w = sb.tile([P, T], U16, name="xt_w", align_bytes=64)
         vs_w = sb.tile([P, S], U16, name="vs_w", align_bytes=64)
         wt_s = sb.tile([P, V], U8, name="wt_s", align_bytes=64)
-        xt_s = sb.tile([P, T], U8, name="xt_s", align_bytes=64)
-        vs_s = sb.tile([P, S], U8, name="vs_s", align_bytes=64)
+        xt_s = sb.tile([P, T], U8, name="xt_s", tag="xt_s", align_bytes=64)
+        vs_s = sb.tile([P, S], U8, name="vs_s", tag="vs_s", align_bytes=64)
         for plane in (wt_s, xt_s, vs_s):
             nc.vector.memset(plane[:].bitcast(I32), 0)
 
@@ -60,19 +60,18 @@ def tile_list_groupgated_chosen_store_plain_kernel(
         for tile, vec in ((sg_t, sg), (bg_t, bg), (sa_t, sa)):
             nc.gpsimd.dma_start(out=tile[:], in_=vec.rearrange("(p t) o -> p (t o)", t=PACK))
 
-        nc.sync.dma_start(l_wt[:], offs)
-        load_scale_rows(nc.sync, wt_s, wt_scales, 0)
-        for q in range(1, QUADS):
-            load_scale_rows(nc.scalar, wt_s, wt_scales, q)
         nc.sync.dma_start(l_xt[:], offs2)
         nc.sync.dma_start(out=xt_w[:].bitcast(I32), in_=xt_words[0].bitcast(I32))
+        nc.sync.dma_start(l_wt[:], offs)
+        for q in range(QUADS):
+            load_scale_rows(nc.scalar if q < 2 else nc.sync, wt_s, wt_scales, q)
         nc.sync.dma_start(out=wt_w[:].bitcast(I32), in_=wt_words[0].rearrange("p n t -> p (n t)").bitcast(I32))
+        nc.sync.dma_start(out=vs_w[:].bitcast(I32), in_=vs_words[0].bitcast(I32))
+        nc.sync.dma_start(l_vs[:], offs5)
         for q in range(QUADS):
             load_scale_rows(nc.sync, xt_s, xt_scales, q)
         nc.sync.dma_start(l_gate[:], offs4)
         nc.sync.dma_start(l_val[:], offs3)
-        nc.sync.dma_start(out=vs_w[:].bitcast(I32), in_=vs_words[0].bitcast(I32))
-        nc.sync.dma_start(l_vs[:], offs5)
         for q in range(QUADS):
             load_scale_rows(nc.sync, vs_s, vs_scales, q)
 
@@ -80,10 +79,13 @@ def tile_list_groupgated_chosen_store_plain_kernel(
         wg_w = sb.tile([P, PACK, P], U32, name="wg_w", align_bytes=64)
         xg_w = sb.tile([P, J], U16, name="xg_w", align_bytes=64)
         xg_s = sb.tile([P, J], U8, name="xg_s", align_bytes=64)
-        nc.vector.tensor_copy(wg_s[:].rearrange("p t q -> p q t"), wt_s[:].indirect(l_wt[:]))
         nc.vector.tensor_copy(xg_w[:], xt_w[:].indirect(l_xt[:]))
+        nc.vector.tensor_copy(wg_s[:].rearrange("p t q -> p q t"), wt_s[:].indirect(l_wt[:]))
         nc.vector.tensor_copy(wg_w[:].rearrange("p t q -> p q t"), wt_w[:].indirect(l_wt[:]))
         nc.vector.tensor_copy(xg_s[:], xt_s[:].indirect(l_xt[:]))
+
+        vg_w = sb.tile([P, N], U16, name="vg_w", tag="xt_s", align_bytes=64)
+        nc.vector.tensor_copy(vg_w[:], vs_w[:].indirect(l_vs[:]))
 
         a_sb = []
         for t in range(PACK):
@@ -101,12 +103,10 @@ def tile_list_groupgated_chosen_store_plain_kernel(
             nc.vector.tensor_copy(a_t[:], a_ps[:])
             a_sb.append(a_t)
 
-        vg_w = sb.tile([P, N], U16, name="vg_w", align_bytes=64)
         vg_s = sb.tile([P, N], U8, name="vg_s", align_bytes=64)
-        nc.vector.tensor_copy(vg_w[:], vs_w[:].indirect(l_vs[:]))
         nc.vector.tensor_copy(vg_s[:], vs_s[:].indirect(l_vs[:]))
 
-        hid = sb.tile([P, O, PACK], BF16, name="hid", align_bytes=64)
+        hid = sb.tile([P, O, PACK], BF16, name="hid", tag="vs_s", align_bytes=64)
         for u in range(2):
             gate = sb.tile([P, 2, O], F32, name=f"gate{u}")
             val = sb.tile([P, 2, O], F32, name=f"val{u}")

@@ -57,11 +57,15 @@ def tile_list_groupgated_chosen_store_plain_kernel(
         sg_t = sb.tile([P, PACK], F32, name="sg_t")
         bg_t = sb.tile([P, PACK], F32, name="bg_t")
         sa_t = sb.tile([P, PACK], F32, name="sa_t")
-        for tile, vec in ((sg_t, sg), (bg_t, bg), (sa_t, sa)):
-            nc.gpsimd.dma_start(out=tile[:], in_=vec.rearrange("(p t) o -> p (t o)", t=PACK))
 
+        def load_row_values(queue, tile, vec):
+            queue.dma_start(out=tile[:], in_=vec.rearrange("(p t) o -> p (t o)", t=PACK))
+
+        load_row_values(nc.gpsimd, sg_t, sg)
+        load_row_values(nc.gpsimd, bg_t, bg)
+
+        nc.scalar.dma_start(out=xt_w[:].bitcast(I32), in_=xt_words[0].bitcast(I32))
         nc.sync.dma_start(l_xt[:], offs2)
-        nc.sync.dma_start(out=xt_w[:].bitcast(I32), in_=xt_words[0].bitcast(I32))
         nc.sync.dma_start(l_wt[:], offs)
         for q in range(QUADS):
             load_scale_rows(nc.scalar if q < 2 else nc.sync, wt_s, wt_scales, q)
@@ -72,6 +76,7 @@ def tile_list_groupgated_chosen_store_plain_kernel(
             load_scale_rows(nc.sync, xt_s, xt_scales, q)
         nc.sync.dma_start(l_gate[:], offs4)
         nc.sync.dma_start(l_val[:], offs3)
+        load_row_values(nc.sync, sa_t, sa)
         for q in range(QUADS):
             load_scale_rows(nc.sync, vs_s, vs_scales, q)
 
@@ -89,18 +94,21 @@ def tile_list_groupgated_chosen_store_plain_kernel(
 
         a_sb = []
         for t in range(PACK):
-            a_ps = ps.tile([P, J], F32, name=f"a_ps{t}")
-            nc.tensor.matmul_mx(
-                out=a_ps[:],
-                lhsT=wg_w[:, t, :].bitcast(E4M3X4),
-                lhsT_scale=wg_s[:, t, :],
-                rhs=xg_w[:].bitcast(E2M1X4),
-                rhs_scale=xg_s[:],
-                start=True,
-                stop=True,
-            )
             a_t = sb.tile([P, J], F32, name=f"a_sb{t}")
-            nc.vector.tensor_copy(a_t[:], a_ps[:])
+            width = J // 2 if t == 0 else J
+            for j0 in range(0, J, width):
+                cols = slice(j0, j0 + width)
+                a_ps = ps.tile([P, width], F32, name=f"a_ps{t}_{j0}")
+                nc.tensor.matmul_mx(
+                    out=a_ps[:],
+                    lhsT=wg_w[:, t, :].bitcast(E4M3X4),
+                    lhsT_scale=wg_s[:, t, :],
+                    rhs=xg_w[:, cols].bitcast(E2M1X4),
+                    rhs_scale=xg_s[:, cols],
+                    start=True,
+                    stop=True,
+                )
+                nc.vector.tensor_copy(a_t[:, cols], a_ps[:])
             a_sb.append(a_t)
 
         vg_s = sb.tile([P, N], U8, name="vg_s", align_bytes=64)

@@ -57,26 +57,21 @@ def tile_list_groupgated_chosen_store_plain_kernel(
         sg_t = sb.tile([P, PACK], F32, name="sg_t")
         bg_t = sb.tile([P, PACK], F32, name="bg_t")
         sa_t = sb.tile([P, PACK], F32, name="sa_t")
+        for tile, vec in ((sg_t, sg), (bg_t, bg), (sa_t, sa)):
+            nc.gpsimd.dma_start(out=tile[:], in_=vec.rearrange("(p t) o -> p (t o)", t=PACK))
 
-        def load_row_values(queue, tile, vec):
-            queue.dma_start(out=tile[:], in_=vec.rearrange("(p t) o -> p (t o)", t=PACK))
-
-        load_row_values(nc.gpsimd, sg_t, sg)
-        load_row_values(nc.gpsimd, bg_t, bg)
-
-        nc.scalar.dma_start(out=xt_w[:].bitcast(I32), in_=xt_words[0].bitcast(I32))
         nc.sync.dma_start(l_xt[:], offs2)
+        nc.sync.dma_start(out=xt_w[:].bitcast(I32), in_=xt_words[0].bitcast(I32))
         nc.sync.dma_start(l_wt[:], offs)
         for q in range(QUADS):
             load_scale_rows(nc.scalar if q < 2 else nc.sync, wt_s, wt_scales, q)
         nc.sync.dma_start(out=wt_w[:].bitcast(I32), in_=wt_words[0].rearrange("p n t -> p (n t)").bitcast(I32))
-        nc.sync.dma_start(out=vs_w[:].bitcast(I32), in_=vs_words[0].bitcast(I32))
-        nc.sync.dma_start(l_vs[:], offs5)
         for q in range(QUADS):
             load_scale_rows(nc.sync, xt_s, xt_scales, q)
         nc.sync.dma_start(l_gate[:], offs4)
+        nc.sync.dma_start(out=vs_w[:].bitcast(I32), in_=vs_words[0].bitcast(I32))
+        nc.sync.dma_start(l_vs[:], offs5)
         nc.sync.dma_start(l_val[:], offs3)
-        load_row_values(nc.sync, sa_t, sa)
         for q in range(QUADS):
             load_scale_rows(nc.sync, vs_s, vs_scales, q)
 

from contextlib import ExitStack

import concourse.mybir as mybir

K, T, J, R, V, O, N, S = 512, 1024, 256, 512, 1024, 128, 256, 1024
FLOPS = 2 * K * R * J + 2 * R * N * O

F32 = mybir.dt.float32
BF16 = mybir.dt.bfloat16
I32 = mybir.dt.int32
U32 = mybir.dt.uint32
U16 = mybir.dt.uint16
U8 = mybir.dt.uint8
E4M3X4 = mybir.dt.float8_e4m3fn_x4
E5M2X4 = mybir.dt.float8_e5m2_x4
E2M1X4 = mybir.dt.float4_e2m1fn_x4
ACT = mybir.ActivationFunctionType
MULT = mybir.AluOpType.mult

P = 128
PACK = 4
QUADS = 4


def tile_list_groupgated_chosen_store_plain_kernel(
    tc, xt_words, xt_scales, wt_words, wt_scales, sa, sg, bg, vs_words, vs_scales, offs, offs2, offs3, offs4, offs5, out
):
    nc = tc.nc
    with ExitStack() as ctx:
        lists = ctx.enter_context(tc.tile_pool(name="lists", bufs=1))
        sb = ctx.enter_context(tc.tile_pool(name="sb", bufs=1))
        ps = ctx.enter_context(tc.psum_pool(name="ps", bufs=1))

        def list_tile(ap, name):
            return lists.tile([P, ap.shape[1]], U16, name=name)

        l_wt = list_tile(offs, "l_wt")
        l_xt = list_tile(offs2, "l_xt")
        l_val = list_tile(offs3, "l_val")
        l_gate = list_tile(offs4, "l_gate")
        l_vs = list_tile(offs5, "l_vs")

        wt_w = sb.tile([P, V], U32, name="wt_w", align_bytes=64)
        xt_w = sb.tile([P, T], U16, name="xt_w", align_bytes=64)
        vs_w = sb.tile([P, S], U16, name="vs_w", align_bytes=64)
        wt_s = sb.tile([P, V], U8, name="wt_s", align_bytes=64)
        xt_s = sb.tile([P, T], U8, name="xt_s", tag="xt_s", align_bytes=64)
        vs_s = sb.tile([P, S], U8, name="vs_s", tag="vs_s", align_bytes=64)
        for plane in (wt_s, xt_s, vs_s):
            nc.vector.memset(plane[:].bitcast(I32), 0)

        def load_scale_rows(queue, plane, scales, q):
            queue.dma_start(
                out=plane[32 * q : 32 * q + 4, :].bitcast(I32), in_=scales[0, 4 * q : 4 * q + 4, :].bitcast(I32)
            )

        sg_t = sb.tile([P, PACK], F32, name="sg_t")
        bg_t = sb.tile([P, PACK], F32, name="bg_t")
        sa_t = sb.tile([P, PACK], F32, name="sa_t")
        for tile, vec in ((sg_t, sg), (bg_t, bg), (sa_t, sa)):
            nc.gpsimd.dma_start(out=tile[:], in_=vec.rearrange("(p t) o -> p (t o)", t=PACK))

        nc.sync.dma_start(l_xt[:], offs2)
        nc.sync.dma_start(out=xt_w[:].bitcast(I32), in_=xt_words[0].bitcast(I32))
        nc.sync.dma_start(l_wt[:], offs)
        for q in range(QUADS):
            load_scale_rows(nc.scalar if q < 2 else nc.sync, wt_s, wt_scales, q)
        nc.sync.dma_start(out=wt_w[:].bitcast(I32), in_=wt_words[0].rearrange("p n t -> p (n t)").bitcast(I32))
        for q in range(QUADS):
            load_scale_rows(nc.sync, xt_s, xt_scales, q)
        nc.sync.dma_start(l_gate[:], offs4)
        nc.sync.dma_start(out=vs_w[:].bitcast(I32), in_=vs_words[0].bitcast(I32))
        nc.sync.dma_start(l_vs[:], offs5)
        nc.sync.dma_start(l_val[:], offs3)
        for q in range(QUADS):
            load_scale_rows(nc.sync, vs_s, vs_scales, q)

        wg_s = sb.tile([P, PACK, P], U8, name="wg_s", align_bytes=64)
        wg_w = sb.tile([P, PACK, P], U32, name="wg_w", align_bytes=64)
        xg_w = sb.tile([P, J], U16, name="xg_w", align_bytes=64)
        xg_s = sb.tile([P, J], U8, name="xg_s", align_bytes=64)
        nc.vector.tensor_copy(xg_w[:], xt_w[:].indirect(l_xt[:]))
        nc.vector.tensor_copy(wg_s[:].rearrange("p t q -> p q t"), wt_s[:].indirect(l_wt[:]))
        nc.vector.tensor_copy(wg_w[:].rearrange("p t q -> p q t"), wt_w[:].indirect(l_wt[:]))
        nc.vector.tensor_copy(xg_s[:], xt_s[:].indirect(l_xt[:]))

        vg_w = sb.tile([P, N], U16, name="vg_w", tag="xt_s", align_bytes=64)
        nc.vector.tensor_copy(vg_w[:], vs_w[:].indirect(l_vs[:]))

        a_sb = []
        for t in range(PACK):
            a_t = sb.tile([P, J], F32, name=f"a_sb{t}")
            width = J // 2 if t == 0 else J
            for j0 in range(0, J, width):
                cols = slice(j0, j0 + width)
                a_ps = ps.tile([P, width], F32, name=f"a_ps{t}_{j0}")
                nc.tensor.matmul_mx(
                    out=a_ps[:],
                    lhsT=wg_w[:, t, :].bitcast(E4M3X4),
                    lhsT_scale=wg_s[:, t, :],
                    rhs=xg_w[:, cols].bitcast(E2M1X4),
                    rhs_scale=xg_s[:, cols],
                    start=True,
                    stop=True,
                )
                nc.vector.tensor_copy(a_t[:, cols], a_ps[:])
            a_sb.append(a_t)

        vg_s = sb.tile([P, N], U8, name="vg_s", align_bytes=64)
        nc.vector.tensor_copy(vg_s[:], vs_s[:].indirect(l_vs[:]))

        hid = sb.tile([P, O, PACK], BF16, name="hid", tag="vs_s", align_bytes=64)
        for u in range(2):
            gate = sb.tile([P, 2, O], F32, name=f"gate{u}")
            val = sb.tile([P, 2, O], F32, name=f"val{u}")
            for e in range(2):
                t = 2 * u + e
                nc.scalar.activation(
                    out=gate[:, e, :], in_=a_sb[t][:].indirect(l_gate[:]), func=ACT.Sigmoid,
                    bias=bg_t[:, t : t + 1], scale=sg_t[:, t : t + 1],
                )
                nc.scalar.activation(
                    out=val[:, e, :], in_=a_sb[t][:].indirect(l_val[:]), func=ACT.Copy, scale=sa_t[:, t : t + 1]
                )
            nc.vector.tensor_tensor(
                hid[:, :, 2 * u : 2 * u + 2],
                val[:].rearrange("p e o -> p o e"),
                gate[:].rearrange("p e o -> p o e"),
                MULT,
            )

        hq_w = sb.tile([P, O], U32, name="hq_w", align_bytes=64)
        hq_s = sb.tile([P, O], U8, name="hq_s", align_bytes=64)
        nc.vector.quantize_mx(out=hq_w[:].bitcast(E5M2X4), scales=hq_s[:], in_=hid[:].rearrange("p o t -> p (o t)"))

        for h in range(N // P):
            cols = slice(h * P, (h + 1) * P)
            y_ps = ps.tile([P, O], F32, name=f"y_ps{h}")
            nc.tensor.matmul_mx(
                out=y_ps[:],
                lhsT=vg_w[:, cols].bitcast(E2M1X4),
                lhsT_scale=vg_s[:, cols],
                rhs=hq_w[:].bitcast(E5M2X4),
                rhs_scale=hq_s[:],
                start=True,
                stop=True,
            )
            y_sb = sb.tile([P, O], F32, name=f"y_sb{h}")
            if h == 0:
                nc.vector.tensor_copy(y_sb[:], y_ps[:])
                nc.sync.dma_start(out=out[cols, :], in_=y_sb[:])
            else:
                nc.scalar.copy(y_sb[:], y_ps[:])
                nc.scalar.dma_start(out=out[cols, :], in_=y_sb[:])
